import numpy as np, ml_dtypes
CORES = [9,13,81,85,89,93,97,101,113,117,121,125]
N = 12
import mx_ref
NC, WT = 256, 1
BF = ml_dtypes.bfloat16
def pk(c, s, i=0):
    return (np.ascontiguousarray(c[:, 512 * i:512 * i + 512]), mx_ref.live(s[:, 128 * i:128 * i + 128]))
def inputs(rng, e, E):
    def f(*shape):
        v = (rng.standard_normal(shape, dtype=np.float32) * np.exp2(rng.integers(-2, 3, shape[:-1] + (1,)))).astype(BF)
        return mx_ref.spread((v.astype(np.float32) * np.exp2(rng.integers(-E, E + 1, shape[:-2] + (1, 1))).astype(np.float32)).astype(BF), rng, e)
    def packed(k):
        c = np.zeros((N, 128, k * 512), np.uint8); s = np.zeros((N, 128, k * 128), np.uint8)
        for r in range(N):
            for i in range(k):
                a, b = mx_ref.quantize(f(128, 512)); c[r][:, 512 * i:512 * i + 512] = a; s[r][:, 128 * i:128 * i + 128] = mx_ref.plane(b, rng)
        return c, s
    d = {}
    d["wc"], d["ws"] = packed(WT)
    d["x"] = f(N, 128, 4 * NC)
    return d
def setup_inputs(rng):
    return inputs(rng, 0, 0)
def setup_inputs_blocks(rng):
    return inputs(rng, 4, 0)
def setup_inputs_wide(rng):
    return inputs(rng, 0, 8)
def reference(wc, ws, x):
    y = np.zeros((N, 128, N * WT * NC), np.float32)
    for r in range(N):
        X = mx_ref.quantize(x[r])
        for b in range(N * WT):
            y[r][:, NC * b:NC * b + NC] = mx_ref.matmul(pk(wc[b // WT], ws[b // WT], b % WT), X)
    return {"y": y}

@@ -1,0 +1,237 @@
+from concourse.bass import DstId, RemoteDMATransfer
+from concourse.mybir import dt, ActivationFunctionType
+
+N = 12
+M = 3
+S = 3
+BANKS = 8
+WW = 128
+XC = 256
+XH = 128
+
+SCRATCH = {
+    "xb": ("sbuf", [128, 4 * XH], "bfloat16"),
+    "xq": ("sbuf", [128, XC], "float8_e4m3fn_x4"),
+    "xs": ("sbuf", [128, XC], "uint8"),
+    "wq": ("sbuf", [128, M * WW], "float8_e4m3fn_x4"),
+    "wp": ("sbuf", [128, M * WW], "uint8"),
+    "st": ("sbuf", [128, S * XC], "float32"),
+    "ps": ("psum", [128, BANKS * 512], "float32"),
+}
+for _j in range(N):
+    SCRATCH["lc%d" % _j] = ("dram", [128, WW], "float8_e4m3fn_x4")
+    SCRATCH["lp%d" % _j] = ("dram", [128, WW], "uint8")
+
+SEMAPHORES = (["arr%d" % j for j in range(N)] + ["fet%d" % s for s in range(M)] + ["mm%d" % s for s in range(M)]
+              + ["cp%d" % t for t in range(S)] + ["sto%d" % t for t in range(S)] + ["ldw", "xl", "xqd", "snt"])
+
+
+def _bits(mask):
+    return [b for b in range(16) if (mask >> b) & 1]
+
+
+def _count(mask):
+    return len(_bits(mask))
+
+
+def _plan(T, topo):
+    cores = [int(c) for c in T.cores]
+    n = len(cores)
+    chips = sorted({topo.chip(c) for c in cores})
+    g0 = [a for a in chips if a == chips[0] or topo.same_plane(a, chips[0])]
+    rest = [a for a in chips if a not in g0]
+    g1 = []
+    for a in g0:
+        m = [b for b in rest if topo.mates(a, b)]
+        g1.append(m[0] if m else None)
+    left = [b for b in rest if b not in g1]
+    g1 = [b if b is not None else (left.pop(0) if left else None) for b in g1]
+    g1 = [b for b in g1 if b is not None] + left
+    idx = {}
+    for grp in (g0, g1):
+        for i, a in enumerate(grp):
+            idx[a] = (i, len(grp))
+
+    def rel(i, q):
+        a, b = cores[i], cores[q]
+        ca, cb = topo.chip(a), topo.chip(b)
+        od = 0 if topo.die(a) == topo.die(b) else 1
+        if i == q:
+            return (0, 0, 0)
+        if ca == cb:
+            return (1, 0, od)
+        d = (idx[cb][0] - idx[ca][0]) % idx[cb][1]
+        if topo.same_plane(ca, cb):
+            return (2, (d - 1) + (idx[cb][1] - 1) * od, od)
+        return (3, d, od)
+
+    order = [sorted(range(n), key=lambda i: rel(i, q) + (i,)) for q in range(n)]
+    every = range(topo.CHIPS * topo.CORES_PER_CHIP)
+    helpers, used = [], set(cores)
+    for i in range(n):
+        far = [cores[q] for q in range(n) if rel(i, q)[0] == 3]
+        cand = [h for h in every if topo.chip(h) == topo.chip(cores[i]) and topo.die(h) == topo.die(cores[i])
+                and h not in used and all(topo.may_write(h, d) for d in far)]
+        helpers.append(cand[:2])
+        used.update(cand[:2])
+    return cores, rel, order, helpers
+
+
+def rank_program(g, core, T, topo):
+    cores, rel, order, helpers = _plan(T, topo)
+    n = len(cores)
+    u8 = dt.uint8
+    sem = T.sem
+
+    def slot_c(s):
+        return T.wq[:, s * WW:(s + 1) * WW]
+
+    def slot_p(s):
+        return T.wp[:, s * WW:(s + 1) * WW]
+
+    def landing(q, j):
+        k = order[q].index(j)
+        if 0 < k < M:
+            return slot_c(k).bitcast(u8), slot_p(k)
+        return T["lc%d" % j][:].bitcast(u8), T["lp%d" % j][:]
+
+    def dram(j):
+        return T["lc%d" % j][:].bitcast(u8), T["lp%d" % j][:]
+
+    def did(c):
+        rid, pid, _ = topo.addr(c)
+        return DstId(rid=rid, pnc=pid)
+
+    def send(j, groups):
+        total = 0
+        for part in (0, 1):
+            trs = []
+            for mask, dests in groups:
+                trs.append(RemoteDMATransfer(dst_ids=[did(c) for c, _ in dests], dma_engine_mask=mask,
+                                             remote_sem=sem["arr%d" % j], srcs=[dram(j)[part]],
+                                             dsts=[ap[part] for _, ap in dests]))
+                total += _count(mask)
+            g.remote_dma_fused(trs, local_sem=sem.snt)
+        return total
+
+    def common(dsts):
+        m = topo.mask(core, dsts[0])
+        for d in dsts[1:]:
+            m &= topo.mask(core, d)
+        return m
+
+    for i in range(n):
+        if core in helpers[i]:
+            h = helpers[i].index(core)
+            nh = len(helpers[i])
+            far = sorted([q for q in range(n) if rel(i, q)[0] == 3], key=lambda q: rel(i, q) + (q,))
+            mine = [q for q in far if rel(i, q)[2] % nh == h]
+            on = common([cores[i]])
+            g.wait_ge(sem["arr%d" % i], 2 * _arrive(topo, cores, i, helpers, rel))
+            m = common([cores[q] for q in mine])
+            tot = send(i, [(m, [(cores[q], landing(q, i)) for q in mine])])
+            g.wait_ge(sem.snt, tot)
+            return
+
+    r = T.rank_of(core)
+    if r is None:
+        return
+
+    g.sync.dma_start(dram(r)[0], T.wc[:]).then_inc(sem.ldw, 16)
+    g.sync.dma_start(dram(r)[1], T.ws[:]).then_inc(sem.ldw, 16)
+    g.scalar.dma_start(T.xb[:], T.x[:, 0:4 * XH]).then_inc(sem.xl, 16)
+    g.sync.dma_start(slot_c(0).bitcast(u8), T.wc[:]).then_inc(sem.fet0, 16)
+    g.sync.dma_start(slot_p(0), T.ws[:]).then_inc(sem.fet0, 16)
+    halves = XC // XH
+    for hx in range(halves):
+        if hx:
+            g.scalar.wait_ge(sem.xqd, hx)
+            g.scalar.dma_start(T.xb[:], T.x[:, 4 * XH * hx:4 * XH * (hx + 1)]).then_inc(sem.xl, 16)
+        g.vector.wait_ge(sem.xl, 16 * (hx + 1))
+        g.vector.quantize_mx(T.xq[:, XH * hx:XH * (hx + 1)], T.xs[:, XH * hx:XH * (hx + 1)], T.xb[:]).then_inc(sem.xqd, 1)
+
+    near = [(h, dram(r)) for h in helpers[r]] + [(cores[q], landing(q, r)) for q in range(n) if rel(r, q)[0] == 1]
+    plane = sorted([q for q in range(n) if rel(r, q)[0] == 2], key=lambda q: rel(r, q) + (q,))
+    off = common([cores[q] for q in plane])
+    onm = common([c for c, _ in near]) & ~off
+    g.wait_ge(sem.ldw, 32)
+    tot = send(r, [(onm, near), (off, [(cores[q], landing(q, r)) for q in plane])])
+
+    got = {}
+    for j in range(n):
+        if j != r:
+            got[j] = 2 * _engines(topo, cores, j, r, helpers, rel)
+
+    fetched = [0] * M
+    fetched[0] = 1
+    for k, j in enumerate(order[r]):
+        s, t, b = k % M, k % S, k % BANKS
+        if k >= M:
+            g.sync.wait_ge(sem["mm%d" % s], k // M)
+            g.sync.wait_ge(sem["arr%d" % j], got[j])
+            g.sync.dma_start(slot_c(s).bitcast(u8), dram(j)[0]).then_inc(sem["fet%d" % s], 16)
+            g.sync.dma_start(slot_p(s), dram(j)[1]).then_inc(sem["fet%d" % s], 16)
+            fetched[s] += 1
+        if k == 0:
+            g.tensor.wait_ge(sem.fet0, 32)
+            g.tensor.wait_ge(sem.xqd, halves)
+        elif k < M:
+            g.tensor.wait_ge(sem["arr%d" % j], got[j])
+        else:
+            g.tensor.wait_ge(sem["fet%d" % s], 32 * fetched[s])
+        if k >= BANKS:
+            kk = k - BANKS
+            g.tensor.wait_ge(sem["cp%d" % (kk % S)], kk // S + 1)
+        g.tensor.matmul_mx(T.ps[:, 512 * b:512 * b + XC], slot_c(s), slot_p(s), T.xq[:], T.xs[:],
+                           True, True).then_inc(sem["mm%d" % s], 1)
+        stage = T.st[:, t * XC:(t + 1) * XC]
+        eng = g.scalar if t == 1 else g.vector
+        eng.wait_ge(sem["mm%d" % s], k // M + 1)
+        if k >= S:
+            eng.wait_ge(sem["sto%d" % t], 16 * (k // S))
+        if t == 1:
+            g.scalar.activation(stage, T.ps[:, 512 * b:512 * b + XC], ActivationFunctionType.Copy).then_inc(sem["cp%d" % t], 1)
+        else:
+            g.vector.tensor_copy(stage, T.ps[:, 512 * b:512 * b + XC]).then_inc(sem["cp%d" % t], 1)
+        g.scalar.wait_ge(sem["cp%d" % t], k // S + 1)
+        g.scalar.dma_start(T.y[:, XC * j:XC * (j + 1)], stage).then_inc(sem["sto%d" % t], 16)
+    for t in range(S):
+        g.scalar.wait_ge(sem["sto%d" % t], 16 * len([k for k in range(n) if k % S == t]))
+    g.wait_ge(sem.snt, tot)
+
+
+def _masks_of_rank(topo, cores, i, helpers, rel):
+    n = len(cores)
+    c = cores[i]
+    off = None
+    for q in range(n):
+        if rel(i, q)[0] == 2:
+            m = topo.mask(c, cores[q])
+            off = m if off is None else off & m
+    on = None
+    for d in list(helpers[i]) + [cores[q] for q in range(n) if rel(i, q)[0] == 1]:
+        m = topo.mask(c, d)
+        on = m if on is None else on & m
+    return on & ~off, off
+
+
+def _arrive(topo, cores, i, helpers, rel):
+    return _count(_masks_of_rank(topo, cores, i, helpers, rel)[0])
+
+
+def _engines(topo, cores, j, q, helpers, rel):
+    kind = rel(j, q)
+    on, off = _masks_of_rank(topo, cores, j, helpers, rel)
+    if kind[0] == 1:
+        return _count(on)
+    if kind[0] == 2:
+        return _count(off)
+    n = len(cores)
+    nh = len(helpers[j])
+    h = helpers[j][kind[2] % nh]
+    m = None
+    for p in range(n):
+        if rel(j, p)[0] == 3 and rel(j, p)[2] % nh == kind[2] % nh:
+            mm = topo.mask(h, cores[p])
+            m = mm if m is None else m & mm
+    return _count(m)

@@ -8,6 +8,7 @@ BANKS = 8
 WW = 128
 XC = 256
 XH = 128
+PB = BANKS // 2
 
 SCRATCH = {
     "xb": ("sbuf", [128, 4 * XH], "bfloat16"),
@@ -22,16 +23,15 @@ for _j in range(N):
     SCRATCH["lc%d" % _j] = ("dram", [128, WW], "float8_e4m3fn_x4")
     SCRATCH["lp%d" % _j] = ("dram", [128, WW], "uint8")
 
-SEMAPHORES = (["arr%d" % j for j in range(N)] + ["fet%d" % s for s in range(M)] + ["mm%d" % s for s in range(M)]
-              + ["cp%d" % t for t in range(S)] + ["sto%d" % t for t in range(S)] + ["ldw", "xl", "xqd", "snt"])
-
-
-def _bits(mask):
-    return [b for b in range(16) if (mask >> b) & 1]
+SEMAPHORES = (["arc%d" % j for j in range(N)] + ["arp%d" % j for j in range(N)]
+              + ["fet%d" % s for s in range(M)] + ["ma%d" % s for s in range(M)] + ["mb%d" % s for s in range(M)]
+              + ["cpv%d" % t for t in range(S)] + ["cps%d" % t for t in range(S)] + ["sto%d" % t for t in range(S)]
+              + ["ldc", "ldp", "xl", "xqd", "snt"])
+ARR = ("arc%d", "arp%d")
 
 
 def _count(mask):
-    return len(_bits(mask))
+    return len([b for b in range(16) if (mask >> b) & 1])
 
 
 def _plan(T, topo):
@@ -63,7 +63,7 @@ def _plan(T, topo):
         d = (idx[cb][0] - idx[ca][0]) % idx[cb][1]
         if topo.same_plane(ca, cb):
             return (2, (d - 1) + (idx[cb][1] - 1) * od, od)
-        return (3, d, od)
+        return (3, d + idx[cb][1] * od, od)
 
     order = [sorted(range(n), key=lambda i: rel(i, q) + (i,)) for q in range(n)]
     every = range(topo.CHIPS * topo.CORES_PER_CHIP)
@@ -77,41 +77,41 @@ def _plan(T, topo):
     return cores, rel, order, helpers
 
 
+def _straight(n, rel, i, cls):
+    return sorted([q for q in range(n) if rel(i, q)[0] == cls and rel(i, q)[2] == 0], key=lambda q: rel(i, q) + (q,))
+
+
 def rank_program(g, core, T, topo):
     cores, rel, order, helpers = _plan(T, topo)
     n = len(cores)
     u8 = dt.uint8
     sem = T.sem
 
-    def slot_c(s):
-        return T.wq[:, s * WW:(s + 1) * WW]
-
-    def slot_p(s):
-        return T.wp[:, s * WW:(s + 1) * WW]
-
-    def landing(q, j):
-        k = order[q].index(j)
-        if 0 < k < M:
-            return slot_c(k).bitcast(u8), slot_p(k)
-        return T["lc%d" % j][:].bitcast(u8), T["lp%d" % j][:]
+    def slot(s):
+        return T.wq[:, s * WW:(s + 1) * WW].bitcast(u8), T.wp[:, s * WW:(s + 1) * WW]
 
     def dram(j):
         return T["lc%d" % j][:].bitcast(u8), T["lp%d" % j][:]
+
+    def direct(q, j):
+        return rel(j, q)[0] == 1 and 0 < order[q].index(j) < M
+
+    def landing(q, j):
+        return slot(order[q].index(j)) if direct(q, j) else dram(j)
 
     def did(c):
         rid, pid, _ = topo.addr(c)
         return DstId(rid=rid, pnc=pid)
 
-    def send(j, groups):
-        total = 0
-        for part in (0, 1):
-            trs = []
-            for mask, dests in groups:
+    def send(j, part, groups):
+        total, trs = 0, []
+        for mask, dests in groups:
+            if dests:
                 trs.append(RemoteDMATransfer(dst_ids=[did(c) for c, _ in dests], dma_engine_mask=mask,
-                                             remote_sem=sem["arr%d" % j], srcs=[dram(j)[part]],
+                                             remote_sem=sem[ARR[part] % j], srcs=[dram(j)[part]],
                                              dsts=[ap[part] for _, ap in dests]))
                 total += _count(mask)
-            g.remote_dma_fused(trs, local_sem=sem.snt)
+        g.remote_dma_fused(trs, local_sem=sem.snt)
         return total
 
     def common(dsts):
@@ -122,14 +122,13 @@ def rank_program(g, core, T, topo):
 
     for i in range(n):
         if core in helpers[i]:
-            h = helpers[i].index(core)
-            nh = len(helpers[i])
-            far = sorted([q for q in range(n) if rel(i, q)[0] == 3], key=lambda q: rel(i, q) + (q,))
-            mine = [q for q in far if rel(i, q)[2] % nh == h]
-            on = common([cores[i]])
-            g.wait_ge(sem["arr%d" % i], 2 * _arrive(topo, cores, i, helpers, rel))
-            m = common([cores[q] for q in mine])
-            tot = send(i, [(m, [(cores[q], landing(q, i)) for q in mine])])
+            mine = _straight(n, rel, i, 3)[helpers[i].index(core)::len(helpers[i])]
+            cnt = _count(_masks_of_rank(topo, cores, i, helpers, rel)[0])
+            grp = [(common([cores[q] for q in mine]), [(cores[q], landing(q, i)) for q in mine])]
+            g.wait_ge(sem[ARR[1] % i], cnt)
+            tot = send(i, 1, grp)
+            g.wait_ge(sem[ARR[0] % i], cnt)
+            tot += send(i, 0, grp)
             g.wait_ge(sem.snt, tot)
             return
 
@@ -137,11 +136,11 @@ def rank_program(g, core, T, topo):
     if r is None:
         return
 
-    g.sync.dma_start(dram(r)[0], T.wc[:]).then_inc(sem.ldw, 16)
-    g.sync.dma_start(dram(r)[1], T.ws[:]).then_inc(sem.ldw, 16)
+    g.sync.dma_start(dram(r)[1], T.ws[:]).then_inc(sem.ldp, 16)
+    g.sync.dma_start(dram(r)[0], T.wc[:]).then_inc(sem.ldc, 16)
     g.scalar.dma_start(T.xb[:], T.x[:, 0:4 * XH]).then_inc(sem.xl, 16)
-    g.sync.dma_start(slot_c(0).bitcast(u8), T.wc[:]).then_inc(sem.fet0, 16)
-    g.sync.dma_start(slot_p(0), T.ws[:]).then_inc(sem.fet0, 16)
+    g.sync.dma_start(slot(0)[0], T.wc[:]).then_inc(sem.fet0, 16)
+    g.sync.dma_start(slot(0)[1], T.ws[:]).then_inc(sem.fet0, 16)
     halves = XC // XH
     for hx in range(halves):
         if hx:
@@ -150,51 +149,79 @@ def rank_program(g, core, T, topo):
         g.vector.wait_ge(sem.xl, 16 * (hx + 1))
         g.vector.quantize_mx(T.xq[:, XH * hx:XH * (hx + 1)], T.xs[:, XH * hx:XH * (hx + 1)], T.xb[:]).then_inc(sem.xqd, 1)
 
-    near = [(h, dram(r)) for h in helpers[r]] + [(cores[q], landing(q, r)) for q in range(n) if rel(r, q)[0] == 1]
-    plane = sorted([q for q in range(n) if rel(r, q)[0] == 2], key=lambda q: rel(r, q) + (q,))
-    off = common([cores[q] for q in plane])
-    onm = common([c for c, _ in near]) & ~off
-    g.wait_ge(sem.ldw, 32)
-    tot = send(r, [(onm, near), (off, [(cores[q], landing(q, r)) for q in plane])])
-
     got = {}
     for j in range(n):
         if j != r:
-            got[j] = 2 * _engines(topo, cores, j, r, helpers, rel)
+            got[j] = _engines(topo, cores, j, r, helpers, rel)
+
+    carry = [(h, dram(r)) for h in helpers[r]]
+    nbq = [q for q in range(n) if rel(r, q)[0] == 1]
+    nbr = [(cores[q], landing(q, r)) for q in nbq]
+    nbr_d = [(cores[q], landing(q, r)) for q in nbq if not direct(q, r)]
+    nbr_s = [(cores[q], landing(q, r)) for q in nbq if direct(q, r)]
+    pl = [(cores[q], landing(q, r)) for q in _straight(n, rel, r, 2)]
+    onm, off = _masks_of_rank(topo, cores, r, helpers, rel)
+    g.wait_ge(sem.ldp, 16)
+    tot = send(r, 1, [(onm, carry + nbr_d), (off, pl)])
+    g.wait_ge(sem.ldc, 16)
+    tot += send(r, 0, [(onm, carry + nbr), (off, pl)])
+    if nbr_s:
+        tot += send(r, 1, [(onm, nbr_s)])
+    for j in order[r]:
+        if rel(j, r)[0] >= 2 and rel(j, r)[2] == 0:
+            onw = [(cores[q], dram(j)) for q in nbq if rel(j, q)[2] == 1]
+            if onw:
+                g.wait_ge(sem[ARR[1] % j], got[j])
+                tot += send(j, 1, [(onm, onw)])
+                g.wait_ge(sem[ARR[0] % j], got[j])
+                tot += send(j, 0, [(onm, onw)])
 
     fetched = [0] * M
     fetched[0] = 1
     for k, j in enumerate(order[r]):
-        s, t, b = k % M, k % S, k % BANKS
-        if k >= M:
-            g.sync.wait_ge(sem["mm%d" % s], k // M)
-            g.sync.wait_ge(sem["arr%d" % j], got[j])
-            g.sync.dma_start(slot_c(s).bitcast(u8), dram(j)[0]).then_inc(sem["fet%d" % s], 16)
-            g.sync.dma_start(slot_p(s), dram(j)[1]).then_inc(sem["fet%d" % s], 16)
+        s, t = k % M, k % S
+        ba, bb = 512 * ((2 * k) % BANKS), 512 * ((2 * k + 1) % BANKS)
+        here = k > 0 and direct(r, j)
+        if k > 0 and not here:
+            if k >= M:
+                g.sync.wait_ge(sem["ma%d" % s], k // M)
+                g.sync.wait_ge(sem["mb%d" % s], k // M)
+            g.sync.wait_ge(sem[ARR[1] % j], got[j])
+            g.sync.wait_ge(sem[ARR[0] % j], got[j])
+            g.sync.dma_start(slot(s)[0], dram(j)[0]).then_inc(sem["fet%d" % s], 16)
+            g.sync.dma_start(slot(s)[1], dram(j)[1]).then_inc(sem["fet%d" % s], 16)
             fetched[s] += 1
         if k == 0:
             g.tensor.wait_ge(sem.fet0, 32)
-            g.tensor.wait_ge(sem.xqd, halves)
-        elif k < M:
-            g.tensor.wait_ge(sem["arr%d" % j], got[j])
+            g.tensor.wait_ge(sem.xqd, 1)
+        elif here:
+            g.tensor.wait_ge(sem[ARR[0] % j], got[j])
+            g.tensor.wait_ge(sem[ARR[1] % j], got[j])
         else:
             g.tensor.wait_ge(sem["fet%d" % s], 32 * fetched[s])
-        if k >= BANKS:
-            kk = k - BANKS
-            g.tensor.wait_ge(sem["cp%d" % (kk % S)], kk // S + 1)
-        g.tensor.matmul_mx(T.ps[:, 512 * b:512 * b + XC], slot_c(s), slot_p(s), T.xq[:], T.xs[:],
-                           True, True).then_inc(sem["mm%d" % s], 1)
-        stage = T.st[:, t * XC:(t + 1) * XC]
-        eng = g.scalar if t == 1 else g.vector
-        eng.wait_ge(sem["mm%d" % s], k // M + 1)
+        wq, wp = T.wq[:, s * WW:(s + 1) * WW], T.wp[:, s * WW:(s + 1) * WW]
+        kk = k - PB
+        if kk >= 0:
+            g.tensor.wait_ge(sem["cpv%d" % (kk % S)], kk // S + 1)
+        g.tensor.matmul_mx(T.ps[:, ba:ba + XH], wq, wp, T.xq[:, 0:XH], T.xs[:, 0:XH],
+                           True, True).then_inc(sem["ma%d" % s], 1)
+        if k == 0:
+            g.tensor.wait_ge(sem.xqd, halves)
+        if kk >= 0:
+            g.tensor.wait_ge(sem["cps%d" % (kk % S)], kk // S + 1)
+        g.tensor.matmul_mx(T.ps[:, bb:bb + XH], wq, wp, T.xq[:, XH:XC], T.xs[:, XH:XC],
+                           True, True).then_inc(sem["mb%d" % s], 1)
+        g.vector.wait_ge(sem["ma%d" % s], k // M + 1)
+        g.scalar.wait_ge(sem["mb%d" % s], k // M + 1)
         if k >= S:
-            eng.wait_ge(sem["sto%d" % t], 16 * (k // S))
-        if t == 1:
-            g.scalar.activation(stage, T.ps[:, 512 * b:512 * b + XC], ActivationFunctionType.Copy).then_inc(sem["cp%d" % t], 1)
-        else:
-            g.vector.tensor_copy(stage, T.ps[:, 512 * b:512 * b + XC]).then_inc(sem["cp%d" % t], 1)
-        g.scalar.wait_ge(sem["cp%d" % t], k // S + 1)
-        g.scalar.dma_start(T.y[:, XC * j:XC * (j + 1)], stage).then_inc(sem["sto%d" % t], 16)
+            g.vector.wait_ge(sem["sto%d" % t], 16 * (k // S))
+            g.scalar.wait_ge(sem["sto%d" % t], 16 * (k // S))
+        g.vector.tensor_copy(T.st[:, t * XC:t * XC + XH], T.ps[:, ba:ba + XH]).then_inc(sem["cpv%d" % t], 1)
+        g.scalar.activation(T.st[:, t * XC + XH:(t + 1) * XC], T.ps[:, bb:bb + XH],
+                            ActivationFunctionType.Copy).then_inc(sem["cps%d" % t], 1)
+        g.scalar.wait_ge(sem["cps%d" % t], k // S + 1)
+        g.scalar.wait_ge(sem["cpv%d" % t], k // S + 1)
+        g.scalar.dma_start(T.y[:, XC * j:XC * (j + 1)], T.st[:, t * XC:(t + 1) * XC]).then_inc(sem["sto%d" % t], 16)
     for t in range(S):
         g.scalar.wait_ge(sem["sto%d" % t], 16 * len([k for k in range(n) if k % S == t]))
     g.wait_ge(sem.snt, tot)
@@ -215,23 +242,22 @@ def _masks_of_rank(topo, cores, i, helpers, rel):
     return on & ~off, off
 
 
-def _arrive(topo, cores, i, helpers, rel):
-    return _count(_masks_of_rank(topo, cores, i, helpers, rel)[0])
-
-
 def _engines(topo, cores, j, q, helpers, rel):
+    n = len(cores)
     kind = rel(j, q)
     on, off = _masks_of_rank(topo, cores, j, helpers, rel)
     if kind[0] == 1:
         return _count(on)
+    if kind[2] == 1:
+        nb = [p for p in range(n) if rel(q, p)[0] == 1 and rel(j, p)[2] == 0][0]
+        return _count(_masks_of_rank(topo, cores, nb, helpers, rel)[0])
     if kind[0] == 2:
         return _count(off)
-    n = len(cores)
+    far = _straight(n, rel, j, 3)
     nh = len(helpers[j])
-    h = helpers[j][kind[2] % nh]
+    hi = far.index(q) % nh
     m = None
-    for p in range(n):
-        if rel(j, p)[0] == 3 and rel(j, p)[2] % nh == kind[2] % nh:
-            mm = topo.mask(h, cores[p])
-            m = mm if m is None else m & mm
+    for p in far[hi::nh]:
+        mm = topo.mask(helpers[j][hi], cores[p])
+        m = mm if m is None else m & mm
     return _count(m)

from concourse.bass import DstId, RemoteDMATransfer
from concourse.mybir import dt, ActivationFunctionType

N = 12
M = 3
S = 3
BANKS = 8
WW = 128
XC = 256
XH = 128
PB = BANKS // 2

SCRATCH = {
    "xb": ("sbuf", [128, 4 * XH], "bfloat16"),
    "xq": ("sbuf", [128, XC], "float8_e4m3fn_x4"),
    "xs": ("sbuf", [128, XC], "uint8"),
    "wq": ("sbuf", [128, M * WW], "float8_e4m3fn_x4"),
    "wp": ("sbuf", [128, M * WW], "uint8"),
    "st": ("sbuf", [128, S * XC], "float32"),
    "ps": ("psum", [128, BANKS * 512], "float32"),
}
for _j in range(N):
    SCRATCH["lc%d" % _j] = ("dram", [128, WW], "float8_e4m3fn_x4")
    SCRATCH["lp%d" % _j] = ("dram", [128, WW], "uint8")

SEMAPHORES = (["arc%d" % j for j in range(N)] + ["arp%d" % j for j in range(N)]
              + ["fet%d" % s for s in range(M)] + ["ma%d" % s for s in range(M)] + ["mb%d" % s for s in range(M)]
              + ["cpv%d" % t for t in range(S)] + ["cps%d" % t for t in range(S)] + ["sto%d" % t for t in range(S)]
              + ["ldc", "ldp", "xl", "xqd", "snt"])
ARR = ("arc%d", "arp%d")


def _count(mask):
    return len([b for b in range(16) if (mask >> b) & 1])


def _plan(T, topo):
    cores = [int(c) for c in T.cores]
    n = len(cores)
    chips = sorted({topo.chip(c) for c in cores})
    g0 = [a for a in chips if a == chips[0] or topo.same_plane(a, chips[0])]
    rest = [a for a in chips if a not in g0]
    g1 = []
    for a in g0:
        m = [b for b in rest if topo.mates(a, b)]
        g1.append(m[0] if m else None)
    left = [b for b in rest if b not in g1]
    g1 = [b if b is not None else (left.pop(0) if left else None) for b in g1]
    g1 = [b for b in g1 if b is not None] + left
    idx = {}
    for grp in (g0, g1):
        for i, a in enumerate(grp):
            idx[a] = (i, len(grp))

    def rel(i, q):
        a, b = cores[i], cores[q]
        ca, cb = topo.chip(a), topo.chip(b)
        od = 0 if topo.die(a) == topo.die(b) else 1
        if i == q:
            return (0, 0, 0)
        if ca == cb:
            return (1, 0, od)
        d = (idx[cb][0] - idx[ca][0]) % idx[cb][1]
        if topo.same_plane(ca, cb):
            return (2, (d - 1) + (idx[cb][1] - 1) * od, od)
        return (3, d + idx[cb][1] * od, od)

    order = [sorted(range(n), key=lambda i: rel(i, q) + (i,)) for q in range(n)]
    every = range(topo.CHIPS * topo.CORES_PER_CHIP)
    helpers, used = [], set(cores)
    for i in range(n):
        far = [cores[q] for q in range(n) if rel(i, q)[0] == 3]
        cand = [h for h in every if topo.chip(h) == topo.chip(cores[i]) and topo.die(h) == topo.die(cores[i])
                and h not in used and all(topo.may_write(h, d) for d in far)]
        helpers.append(cand[:2])
        used.update(cand[:2])
    return cores, rel, order, helpers


def _straight(n, rel, i, cls):
    return sorted([q for q in range(n) if rel(i, q)[0] == cls and rel(i, q)[2] == 0], key=lambda q: rel(i, q) + (q,))


def rank_program(g, core, T, topo):
    cores, rel, order, helpers = _plan(T, topo)
    n = len(cores)
    u8 = dt.uint8
    sem = T.sem

    def slot(s):
        return T.wq[:, s * WW:(s + 1) * WW].bitcast(u8), T.wp[:, s * WW:(s + 1) * WW]

    def dram(j):
        return T["lc%d" % j][:].bitcast(u8), T["lp%d" % j][:]

    def direct(q, j):
        return rel(j, q)[0] == 1 and 0 < order[q].index(j) < M

    def landing(q, j):
        return slot(order[q].index(j)) if direct(q, j) else dram(j)

    def did(c):
        rid, pid, _ = topo.addr(c)
        return DstId(rid=rid, pnc=pid)

    def send(j, part, groups):
        total, trs = 0, []
        for mask, dests in groups:
            if dests:
                trs.append(RemoteDMATransfer(dst_ids=[did(c) for c, _ in dests], dma_engine_mask=mask,
                                             remote_sem=sem[ARR[part] % j], srcs=[dram(j)[part]],
                                             dsts=[ap[part] for _, ap in dests]))
                total += _count(mask)
        g.remote_dma_fused(trs, local_sem=sem.snt)
        return total

    def common(dsts):
        m = topo.mask(core, dsts[0])
        for d in dsts[1:]:
            m &= topo.mask(core, d)
        return m

    for i in range(n):
        if core in helpers[i]:
            mine = _straight(n, rel, i, 3)[helpers[i].index(core)::len(helpers[i])]
            cnt = _count(_masks_of_rank(topo, cores, i, helpers, rel)[0])
            grp = [(common([cores[q] for q in mine]), [(cores[q], landing(q, i)) for q in mine])]
            g.wait_ge(sem[ARR[1] % i], cnt)
            tot = send(i, 1, grp)
            g.wait_ge(sem[ARR[0] % i], cnt)
            tot += send(i, 0, grp)
            g.wait_ge(sem.snt, tot)
            return

    r = T.rank_of(core)
    if r is None:
        return

    g.sync.dma_start(dram(r)[1], T.ws[:]).then_inc(sem.ldp, 16)
    g.sync.dma_start(dram(r)[0], T.wc[:]).then_inc(sem.ldc, 16)
    g.scalar.dma_start(T.xb[:], T.x[:, 0:4 * XH]).then_inc(sem.xl, 16)
    g.sync.dma_start(slot(0)[0], T.wc[:]).then_inc(sem.fet0, 16)
    g.sync.dma_start(slot(0)[1], T.ws[:]).then_inc(sem.fet0, 16)
    halves = XC // XH
    for hx in range(halves):
        if hx:
            g.scalar.wait_ge(sem.xqd, hx)
            g.scalar.dma_start(T.xb[:], T.x[:, 4 * XH * hx:4 * XH * (hx + 1)]).then_inc(sem.xl, 16)
        g.vector.wait_ge(sem.xl, 16 * (hx + 1))
        g.vector.quantize_mx(T.xq[:, XH * hx:XH * (hx + 1)], T.xs[:, XH * hx:XH * (hx + 1)], T.xb[:]).then_inc(sem.xqd, 1)

    got = {}
    for j in range(n):
        if j != r:
            got[j] = _engines(topo, cores, j, r, helpers, rel)

    carry = [(h, dram(r)) for h in helpers[r]]
    nbq = [q for q in range(n) if rel(r, q)[0] == 1]
    nbr = [(cores[q], landing(q, r)) for q in nbq]
    nbr_d = [(cores[q], landing(q, r)) for q in nbq if not direct(q, r)]
    nbr_s = [(cores[q], landing(q, r)) for q in nbq if direct(q, r)]
    pl = [(cores[q], landing(q, r)) for q in _straight(n, rel, r, 2)]
    onm, off = _masks_of_rank(topo, cores, r, helpers, rel)
    g.wait_ge(sem.ldp, 16)
    tot = send(r, 1, [(onm, carry + nbr_d), (off, pl)])
    g.wait_ge(sem.ldc, 16)
    tot += send(r, 0, [(onm, carry + nbr), (off, pl)])
    if nbr_s:
        tot += send(r, 1, [(onm, nbr_s)])
    for j in order[r]:
        if rel(j, r)[0] >= 2 and rel(j, r)[2] == 0:
            onw = [(cores[q], dram(j)) for q in nbq if rel(j, q)[2] == 1]
            if onw:
                g.wait_ge(sem[ARR[1] % j], got[j])
                tot += send(j, 1, [(onm, onw)])
                g.wait_ge(sem[ARR[0] % j], got[j])
                tot += send(j, 0, [(onm, onw)])

    fetched = [0] * M
    fetched[0] = 1
    for k, j in enumerate(order[r]):
        s, t = k % M, k % S
        ba, bb = 512 * ((2 * k) % BANKS), 512 * ((2 * k + 1) % BANKS)
        here = k > 0 and direct(r, j)
        if k > 0 and not here:
            if k >= M:
                g.sync.wait_ge(sem["ma%d" % s], k // M)
                g.sync.wait_ge(sem["mb%d" % s], k // M)
            g.sync.wait_ge(sem[ARR[1] % j], got[j])
            g.sync.wait_ge(sem[ARR[0] % j], got[j])
            g.sync.dma_start(slot(s)[0], dram(j)[0]).then_inc(sem["fet%d" % s], 16)
            g.sync.dma_start(slot(s)[1], dram(j)[1]).then_inc(sem["fet%d" % s], 16)
            fetched[s] += 1
        if k == 0:
            g.tensor.wait_ge(sem.fet0, 32)
            g.tensor.wait_ge(sem.xqd, 1)
        elif here:
            g.tensor.wait_ge(sem[ARR[0] % j], got[j])
            g.tensor.wait_ge(sem[ARR[1] % j], got[j])
        else:
            g.tensor.wait_ge(sem["fet%d" % s], 32 * fetched[s])
        wq, wp = T.wq[:, s * WW:(s + 1) * WW], T.wp[:, s * WW:(s + 1) * WW]
        kk = k - PB
        if kk >= 0:
            g.tensor.wait_ge(sem["cpv%d" % (kk % S)], kk // S + 1)
        g.tensor.matmul_mx(T.ps[:, ba:ba + XH], wq, wp, T.xq[:, 0:XH], T.xs[:, 0:XH],
                           True, True).then_inc(sem["ma%d" % s], 1)
        if k == 0:
            g.tensor.wait_ge(sem.xqd, halves)
        if kk >= 0:
            g.tensor.wait_ge(sem["cps%d" % (kk % S)], kk // S + 1)
        g.tensor.matmul_mx(T.ps[:, bb:bb + XH], wq, wp, T.xq[:, XH:XC], T.xs[:, XH:XC],
                           True, True).then_inc(sem["mb%d" % s], 1)
        g.vector.wait_ge(sem["ma%d" % s], k // M + 1)
        g.scalar.wait_ge(sem["mb%d" % s], k // M + 1)
        if k >= S:
            g.vector.wait_ge(sem["sto%d" % t], 16 * (k // S))
            g.scalar.wait_ge(sem["sto%d" % t], 16 * (k // S))
        g.vector.tensor_copy(T.st[:, t * XC:t * XC + XH], T.ps[:, ba:ba + XH]).then_inc(sem["cpv%d" % t], 1)
        g.scalar.activation(T.st[:, t * XC + XH:(t + 1) * XC], T.ps[:, bb:bb + XH],
                            ActivationFunctionType.Copy).then_inc(sem["cps%d" % t], 1)
        g.scalar.wait_ge(sem["cps%d" % t], k // S + 1)
        g.scalar.wait_ge(sem["cpv%d" % t], k // S + 1)
        g.scalar.dma_start(T.y[:, XC * j:XC * (j + 1)], T.st[:, t * XC:(t + 1) * XC]).then_inc(sem["sto%d" % t], 16)
    for t in range(S):
        g.scalar.wait_ge(sem["sto%d" % t], 16 * len([k for k in range(n) if k % S == t]))
    g.wait_ge(sem.snt, tot)


def _masks_of_rank(topo, cores, i, helpers, rel):
    n = len(cores)
    c = cores[i]
    off = None
    for q in range(n):
        if rel(i, q)[0] == 2:
            m = topo.mask(c, cores[q])
            off = m if off is None else off & m
    on = None
    for d in list(helpers[i]) + [cores[q] for q in range(n) if rel(i, q)[0] == 1]:
        m = topo.mask(c, d)
        on = m if on is None else on & m
    return on & ~off, off


def _engines(topo, cores, j, q, helpers, rel):
    n = len(cores)
    kind = rel(j, q)
    on, off = _masks_of_rank(topo, cores, j, helpers, rel)
    if kind[0] == 1:
        return _count(on)
    if kind[2] == 1:
        nb = [p for p in range(n) if rel(q, p)[0] == 1 and rel(j, p)[2] == 0][0]
        return _count(_masks_of_rank(topo, cores, nb, helpers, rel)[0])
    if kind[0] == 2:
        return _count(off)
    far = _straight(n, rel, j, 3)
    nh = len(helpers[j])
    hi = far.index(q) % nh
    m = None
    for p in far[hi::nh]:
        mm = topo.mask(helpers[j][hi], cores[p])
        m = mm if m is None else m & mm
    return _count(m)
